import numpy as np, ml_dtypes
CORES = [2,6,26,30,66,70,74,78,82,86]
N = 10
KB, QP = 1, 256
MEM = [3,9]
WID = [96,32,96,192,32,256,96,96,96,224]
def setup_inputs(rng):
    return {"q": rng.standard_normal((N, 128, QP), dtype=np.float32).astype(ml_dtypes.bfloat16), "k": rng.standard_normal((N, 128, KB * 128), dtype=np.float32).astype(ml_dtypes.bfloat16), "v": rng.standard_normal((N, 128, KB * 128), dtype=np.float32).astype(ml_dtypes.bfloat16)}
def setup_inputs_big(rng):
    d = setup_inputs(rng)
    for k in ("q", "k", "v"): d[k] = (d[k].astype(np.float32) * 1024.0).astype(d[k].dtype)
    return d
def setup_inputs_small(rng):
    d = setup_inputs(rng)
    for k in ("q", "k", "v"): d[k] = (d[k].astype(np.float32) * (1 / 1024.0)).astype(d[k].dtype)
    return d
def setup_inputs_apart(rng):
    d = setup_inputs(rng)
    f = (10.0 ** rng.permutation(np.linspace(-1.5, 1.5, N))).astype(np.float32).reshape(N, 1, 1)
    for k in ("q", "k", "v"): d[k] = (d[k].astype(np.float32) * f).astype(d[k].dtype)
    return d
def whole(q, k, v):
    Q, K, V = q.astype(np.float64), k.astype(np.float64), v.astype(np.float64)
    y = np.zeros((N, 128, QP))
    for r in range(N):
        for j in MEM:
            for b in range(KB):
                S = np.maximum(K[j][:, 128 * b:128 * b + 128].T @ Q[r], 0.0)
                y[r] += V[j][:, 128 * b:128 * b + 128].T @ S
    return {"y": y.astype(ml_dtypes.bfloat16 if q.dtype != np.float64 else np.float64)}
def reference(q, k, v):
    o = whole(q, k, v)["y"].copy()
    for r in range(N):
        o[r][:, WID[r]:] = np.nan
    return {"y": o}

from concourse.bass import DstId, RemoteDMATransfer
from concourse.mybir import AluOpType

KP = 128
QP = 256
NSPLIT = 2
ROUND = 2

SCRATCH = {
    "kv0": ("sbuf", [128, 2 * KP], "bfloat16"),
    "kv1": ("sbuf", [128, 2 * KP], "bfloat16"),
    "qo": ("sbuf", [128, QP], "bfloat16"),
    "qs": ("sbuf", [128, QP], "bfloat16"),
    "zero": ("sbuf", [128, QP], "bfloat16"),
    "sa": ("sbuf", [128, QP], "bfloat16"),
    "sb": ("sbuf", [128, QP], "bfloat16"),
    "osend": ("sbuf", [128, QP], "bfloat16"),
    "orecv": ("sbuf", [128, QP], "bfloat16"),
    "yo": ("sbuf", [128, QP], "bfloat16"),
    "p1a": ("psum", [128, 512], "float32"),
    "p1b": ("psum", [128, 512], "float32"),
    "p2a": ("psum", [128, 512], "float32"),
    "p2b": ("psum", [128, 512], "float32"),
}
SEMAPHORES = ["kvl", "ql", "zs", "kva0", "kva1", "qa", "m1a", "m1b", "m2a", "m2b", "rla", "rlb", "oc", "oa", "yd",
              "st", "sent"]


def _hops(topo, a, b):
    ca, cb = topo.chip(a), topo.chip(b)
    if ca == cb:
        return 0
    return 1 if (topo.mates(ca, cb) or topo.same_plane(ca, cb)) else 2


def _bits(mask):
    return [b for b in range(mask.bit_length()) if (mask >> b) & 1]


def _mask(bits):
    m = 0
    for b in bits:
        m |= 1 << b
    return m


def _plan(T, topo):
    cores, mem, wid = list(T.cores), list(T.tables["MEM"]), list(T.tables["WID"])
    chips = {}
    for r, c in enumerate(cores):
        chips.setdefault(topo.chip(c), []).append(r)
    sib = {}
    for rs in chips.values():
        sib[rs[0]], sib[rs[1]] = rs[1], rs[0]
    free = [ch for ch, rs in chips.items() if not [r for r in rs if r in mem]]
    free.sort(key=lambda ch: max(wid[r] for r in chips[ch]))
    split = free[:NSPLIT]
    holds = {}
    for ch, rs in chips.items():
        if ch in split:
            a, b = rs
            heavy = a if wid[b] >= wid[a] else b
            near = sorted(range(len(mem)), key=lambda i: _hops(topo, cores[mem[i]], cores[heavy]))
            holds[heavy], holds[sib[heavy]] = [near[0]], [near[1]]
        else:
            for r in rs:
                holds[r] = sorted(range(len(mem)), key=lambda i: _hops(topo, cores[mem[i]], cores[r]))
    rounds, gets = {}, {}
    for i, j in enumerate(mem):
        src = cores[j]
        want = [r for r in range(len(cores)) if r != j and i in holds[r]]
        far = [r for r in want if topo.chip(cores[r]) != topo.chip(src)]
        home = [r for r in want if topo.chip(cores[r]) == topo.chip(src)]
        far.sort(key=lambda r: (len(holds[r]), -wid[r]))
        out = _bits(topo.mask(src, cores[far[0]]))
        calls = []
        for n in range(0, len(far), ROUND):
            grp = far[n:n + ROUND]
            e = len(out) // len(grp)
            calls.append([(r, _mask(out[x * e:(x + 1) * e]), e) for x, r in enumerate(grp)])
        for r in home:
            stay = [b for b in _bits(topo.mask(src, cores[r])) if b not in out]
            calls[-1].append((r, _mask(stay), len(stay)))
        rounds[i] = calls
        for call in calls:
            for r, _m, e in call:
                gets[(i, r)] = e
    return cores, mem, wid, sib, holds, rounds, gets


def rank_program(g, core, T, topo):
    rank = T.rank_of(core)
    if rank is None:
        return
    cores, mem, wid, sib, holds, rounds, gets = _plan(T, topo)
    S = T.sem
    W = wid[rank]
    mine = mem.index(rank) if rank in mem else None
    kv = [T.kv0, T.kv1]
    kva = [S.kva0, S.kva1]
    sent = 0

    def kv_wait(queue, i):
        if i == mine:
            queue.wait_ge(S.kvl, 32)
        else:
            queue.wait_ge(kva[i], gets[(i, rank)])

    if mine is not None:
        g.sync.dma_start(kv[mine][:, 0:KP], T.k[:, :]).then_inc(S.kvl, 16)
        g.scalar.dma_start(kv[mine][:, KP:2 * KP], T.v[:, :]).then_inc(S.kvl, 16)
    g.sync.dma_start(T.qo[:, 0:W], T.q[:, 0:W]).then_inc(S.ql, 16)
    g.vector.memset(T.zero[:, :], 0.0).then_inc(S.zs, 1)
    g.vector.wait_ge(S.zs, 1)

    if mine is not None:
        g.wait_ge(S.kvl, 32)
        for call in rounds[mine]:
            trs = []
            for r, m, e in call:
                rid, pid, _se = topo.addr(cores[r])
                trs.append(RemoteDMATransfer(dst_ids=[DstId(rid=rid, pnc=pid)], dma_engine_mask=m,
                                             remote_sem=kva[mine], src=kv[mine][:, :], dst=kv[mine][:, :]))
                sent += e
            g.remote_dma_fused(trs, local_sem=S.sent)

    if len(holds[rank]) > 1:
        a, b = holds[rank]
        g.tensor.wait_ge(S.ql, 16)
        kv_wait(g.tensor, a)
        g.tensor.matmul(T.p1a[:, 0:W], kv[a][:, 0:KP], T.qo[:, 0:W], True, True).then_inc(S.m1a, 1)
        kv_wait(g.tensor, b)
        g.tensor.matmul(T.p1b[:, 0:W], kv[b][:, 0:KP], T.qo[:, 0:W], True, True).then_inc(S.m1b, 1)
        g.tensor.wait_ge(S.rla, 1)
        g.tensor.matmul(T.p2a[:, 0:W], kv[a][:, KP:2 * KP], T.sa[:, 0:W], True, False)
        g.tensor.wait_ge(S.rlb, 1)
        g.tensor.matmul(T.p2a[:, 0:W], kv[b][:, KP:2 * KP], T.sb[:, 0:W], False, True).then_inc(S.m2a, 1)

        g.vector.wait_ge(S.m1a, 1)
        g.vector.tensor_tensor(T.sa[:, 0:W], T.p1a[:, 0:W], T.zero[:, 0:W], AluOpType.max).then_inc(S.rla, 1)
        g.vector.wait_ge(S.m1b, 1)
        g.vector.tensor_tensor(T.sb[:, 0:W], T.p1b[:, 0:W], T.zero[:, 0:W], AluOpType.max).then_inc(S.rlb, 1)
        g.vector.wait_ge(S.m2a, 1)
        g.vector.tensor_copy(T.yo[:, 0:W], T.p2a[:, 0:W]).then_inc(S.yd, 1)
    else:
        i = holds[rank][0]
        mate = sib[rank]
        Wp = wid[mate]
        rid, pid, _se = topo.addr(cores[mate])
        on = _bits(topo.mask(core, cores[mate]))
        if mine is not None:
            busy = [b for call in rounds[mine] for _r, m, _e in call for b in _bits(m)]
            on = [b for b in on if b not in busy]
        g.wait_ge(S.ql, 16)
        g.remote_dma(out_ap=T.qs[:, 0:W], in_ap=T.qo[:, 0:W], remote_sem=S.qa, local_sem=S.sent, pid=pid,
                     routing_id=rid, dma_engine_mask=_mask(on))
        sent += len(on)
        there = _bits(topo.mask(cores[mate], core))
        if mate in mem:
            far = [b for call in rounds[mem.index(mate)] for _r, m, _e in call for b in _bits(m)]
            there = [b for b in there if b not in far]

        kv_wait(g.tensor, i)
        g.tensor.wait_ge(S.qa, len(there))
        g.tensor.matmul(T.p1a[:, 0:Wp], kv[i][:, 0:KP], T.qs[:, 0:Wp], True, True).then_inc(S.m1a, 1)
        g.tensor.wait_ge(S.ql, 16)
        g.tensor.matmul(T.p1b[:, 0:W], kv[i][:, 0:KP], T.qo[:, 0:W], True, True).then_inc(S.m1b, 1)
        g.tensor.wait_ge(S.rla, 1)
        g.tensor.matmul(T.p2a[:, 0:Wp], kv[i][:, KP:2 * KP], T.sa[:, 0:Wp], True, True).then_inc(S.m2a, 1)
        g.tensor.wait_ge(S.rlb, 1)
        g.tensor.matmul(T.p2b[:, 0:W], kv[i][:, KP:2 * KP], T.sb[:, 0:W], True, True).then_inc(S.m2b, 1)

        g.vector.wait_ge(S.m1a, 1)
        g.vector.tensor_tensor(T.sa[:, 0:Wp], T.p1a[:, 0:Wp], T.zero[:, 0:Wp], AluOpType.max).then_inc(S.rla, 1)
        g.vector.wait_ge(S.m2a, 1)
        g.vector.tensor_copy(T.osend[:, 0:Wp], T.p2a[:, 0:Wp]).then_inc(S.oc, 1)
        g.vector.wait_ge(S.m1b, 1)
        g.vector.tensor_tensor(T.sb[:, 0:W], T.p1b[:, 0:W], T.zero[:, 0:W], AluOpType.max).then_inc(S.rlb, 1)

        g.wait_ge(S.oc, 1)
        g.remote_dma(out_ap=T.orecv[:, 0:Wp], in_ap=T.osend[:, 0:Wp], remote_sem=S.oa, local_sem=S.sent, pid=pid,
                     routing_id=rid, dma_engine_mask=_mask(on))
        sent += len(on)

        g.vector.wait_ge(S.m2b, 1)
        g.vector.wait_ge(S.oa, len(there))
        g.vector.tensor_tensor(T.yo[:, 0:W], T.p2b[:, 0:W], T.orecv[:, 0:W], AluOpType.add).then_inc(S.yd, 1)

    g.sync.wait_ge(S.yd, 1)
    g.sync.dma_start(T.y[:, 0:W], T.yo[:, 0:W]).then_inc(S.st, 16)
    g.sync.wait_ge(S.st, 16)
    if sent:
        g.wait_ge(S.sent, sent)
